import numpy as np
import ml_dtypes


def mxq(x, axis, fmt="e4m3"):
    dtype, down = {"e4m3": (ml_dtypes.float8_e4m3fn, 7), "e5m2": (ml_dtypes.float8_e5m2, 14)}[fmt]
    v = np.moveaxis(np.asarray(x, np.float32).astype(ml_dtypes.bfloat16).astype(np.float64), axis, -1)
    blocks = v.reshape(v.shape[:-1] + (-1, 32))
    amax = np.abs(blocks).max(-1, keepdims=True)
    byte = np.maximum(np.where(amax > 0, np.frexp(amax)[1] - 1 + 127, 0) - down, 1)
    scale = np.exp2(byte - 127.0)
    codes = (blocks / scale).astype(np.float32).astype(dtype).astype(np.float64)
    return np.moveaxis((codes * scale).reshape(v.shape), -1, axis)


WIDE = False


def mx_kscale(k):
    if not WIDE:
        return np.ones(k)
    levels = np.array([10, -10, 5, -5, 0])
    if k % 512:
        return np.exp2(np.random.permutation(np.resize(levels, k // 32))).repeat(32)
    a = np.empty((k // 512, 16))
    for p in range(k // 512):
        a[p, :8] = np.random.permutation(np.resize(levels, 8))
        for g in range(8):
            far = levels[np.abs(levels - a[p, g]) >= 10]
            a[p, g + 8] = far[np.random.randint(len(far))]
    return np.exp2(a.ravel()).repeat(32)


def f64(x):
    return np.asarray(x).astype(np.float64)


def striped(idx):
    return np.tile(idx.reshape(-1, 16).T, (8, 1)).astype(np.uint16)


def unstriped(offs):
    return offs[:16].T.reshape(-1).astype(np.int64)


def striped8(idx):
    return np.concatenate([x.reshape(-1, 16).T for x in idx]).astype(np.uint16)


def runs(offs, k):
    lists = np.stack([offs[16 * r : 16 * r + 16].T.reshape(-1) for r in range(8)]).astype(np.int64)
    return lists[np.arange(k) % 512 // 64]


def pack_weight(w):
    k, n = w.shape
    w = f64(np.asarray(w, np.float32).astype(ml_dtypes.bfloat16)).reshape(k // 32, 32, n)
    amax = np.abs(w).max(1)
    byte = np.clip(np.where(amax > 0, np.frexp(amax)[1] - 1 + 127 - 7, 1), 1, 254)
    scaled = (w * np.exp2(127.0 - byte)[:, None, :]).reshape(k, n).astype(np.float32)
    words = np.ascontiguousarray(scaled.reshape(k // 512, 128, 4, n).transpose(0, 1, 3, 2)).astype(ml_dtypes.float8_e4m3fn).view(np.uint8)
    return words, np.ascontiguousarray(byte.astype(np.uint8).reshape(k // 512, 16, n))


def unpack_weight(words, scales):
    g, p, n, _ = words.shape
    vals = np.ascontiguousarray(words).view(ml_dtypes.float8_e4m3fn).astype(np.float64) * np.repeat(np.exp2(scales.astype(np.float64) - 127.0), 8, axis=1)[..., None]
    return vals.transpose(0, 1, 3, 2).reshape(g * 512, n)


def sigmoid(v):
    return 1.0 / (1.0 + np.exp(-np.maximum(v, -700.0)))

def planes(y):
    n, m = y.shape
    v = y.astype(np.float32).astype(ml_dtypes.bfloat16).astype(np.float64).reshape(n // 32, 32, m)
    top = np.abs(v).max(1)
    byte = np.clip(np.where(top > 0, np.frexp(top)[1] - 1 + 127 - 7, 1), 1, 254)
    codes = (v * np.exp2(127.0 - byte)[:, None, :]).reshape(n, m).astype(np.float32).astype(ml_dtypes.float8_e4m3fn).view(np.uint8)
    words = codes.reshape(n // 512, 128, 4, m).transpose(0, 1, 3, 2)
    return np.ascontiguousarray(words), np.ascontiguousarray(byte.astype(np.uint8).reshape(n // 512, 16, m))


K, T, S, N, H, U = 512, 2048, 512, 512, 512, 1024


def setup_inputs():
    n = np.random.standard_normal
    s = mx_kscale(K)[:, None]
    u = mx_kscale(H)
    packed_xT = pack_weight(n((K, T)) * s)
    packed_w1 = pack_weight(n((K, H)) / np.sqrt(K) / s)
    packed_w2 = pack_weight(n((K, H)) / np.sqrt(K) / s)
    packed_w3 = pack_weight(n((H, N)) / np.sqrt(H) / u[:, None])
    return {
        "x_words": packed_xT[0],
        "x_scales": packed_xT[1],
        "w1_words": packed_w1[0],
        "w1_scales": packed_w1[1],
        "w2_words": packed_w2[0],
        "w2_scales": packed_w2[1],
        "gn": (np.random.uniform(0.5, 1.5, (H, 1)) * u[:, None]).astype(np.float32),
        "w3_words": packed_w3[0],
        "w3_scales": packed_w3[1],
        "mem": n((N, U)).astype(np.float32),
        "offs": striped(np.random.permutation(T)[:S]),
        "two": striped(np.random.permutation(T)[:S]),
        "t1": striped8(np.stack([np.random.permutation(S) for _ in range(8)])),
        "t2": striped8(np.stack([np.random.permutation(S) for _ in range(8)])),
        "t3": striped8(np.stack([np.random.permutation(S) for _ in range(8)])),
        "slot": striped8(np.stack([np.random.permutation(U)[:S] for _ in range(8)])),
    }


def reference(x_words, x_scales, w1_words, w1_scales, w2_words, w2_scales, gn, w3_words, w3_scales, mem, offs, two, t1, t2, t3, slot):
    x_two = unpack_weight(x_words, x_scales)[:, unstriped(two)]
    c = unpack_weight(w2_words, w2_scales).T @ x_two
    xq = unpack_weight(x_words, x_scales)[:, unstriped(offs)]
    y = unpack_weight(w1_words, w1_scales).T @ xq
    z = f64(gn) * (1.0 * (sigmoid(3.0 * (c - (y[np.arange(H)[:, None], runs(t1, H)]))) + sigmoid(3.0 * (c - (y[np.arange(H)[:, None], runs(t2, H)]))) + sigmoid(3.0 * (c - (y[np.arange(H)[:, None], runs(t3, H)])))) + -1.5)
    h = unpack_weight(w3_words, w3_scales).T @ mxq(z, 0, "e4m3")
    out = f64(mem).copy()
    out[np.arange(N)[:, None], runs(slot, N)] = h
    return (out,) + planes(out)

@@ -1,0 +1,278 @@
+from contextlib import ExitStack
+
+import concourse.mybir as mybir
+from concourse.masks import make_identity
+
+F32 = mybir.dt.float32
+BF16 = mybir.dt.bfloat16
+U32 = mybir.dt.uint32
+I32 = mybir.dt.int32
+U16 = mybir.dt.uint16
+U8 = mybir.dt.uint8
+FP8X4 = mybir.dt.float8_e4m3fn_x4
+ACT = mybir.ActivationFunctionType
+ALU = mybir.AluOpType
+
+K, T, S, N, H, U = 512, 2048, 512, 512, 512, 1024
+FLOPS = 2 * (K * H * S * 2 + H * N * S)
+
+P = 128
+PACK = 4
+BLK = 128
+NBLK = S // BLK
+TAPS = 3
+COLS = BLK // 16
+NQ = 4
+QW = U // NQ
+VECTOR_TRIOS = 10
+FETCH_AFTER = {(b, t): "f%d_%d" % (b, t) for b in range(4) for t in range(4)}
+V_AFTER = {0: "first", 1: "neg_c0", 2: "z0"}
+
+
+def tile_picked_shadowpcf_none_po_kernel(tc, x_words, x_scales, w1_words, w1_scales, w2_words, w2_scales, gn, w3_words, w3_scales, mem, offs, two, t1, t2, t3, slot, out_0, out_1, out_2):
+    nc = tc.nc
+
+    def word_rows(words):
+        return words[0].rearrange("p n r -> p (n r)").bitcast(I32)
+
+    with ExitStack() as ctx:
+        lists = ctx.enter_context(tc.tile_pool(name="lists", bufs=1))
+        keep = ctx.enter_context(tc.tile_pool(name="keep", bufs=1))
+        psum = ctx.enter_context(tc.psum_pool(name="psum", bufs=1))
+
+        offs_l = lists.tile([P, S // 16], U16, name="offs_l")
+        two_l = lists.tile([P, S // 16], U16, name="two_l")
+        tap_l = [lists.tile([P, S // 16], U16, name="tap_l%d" % k) for k in range(TAPS)]
+        slot_l = lists.tile([P, S // 16], U16, name="slot_l")
+
+        xs = keep.tile([P, T], U8, name="xs", tag="page3", align_bytes=64)
+        xw = keep.tile([P, T], I32, name="xw", tag="page0", align_bytes=64)
+        w1_raw = keep.tile([P, H], I32, name="w1_raw", tag="page1", align_bytes=64)
+        w2_raw = keep.tile([P, H], I32, name="w2_raw", tag="page2", align_bytes=64)
+        w3_raw = keep.tile([P, N], I32, name="w3_raw", align_bytes=64)
+        gain = keep.tile([P, PACK], F32, name="gain")
+        half_gain = keep.tile([P, PACK], F32, name="half_gain")
+        ident = keep.tile([P, P], F32, name="ident")
+        ws12_raw = keep.tile([P, H], U8, name="ws12_raw", tag="ws12_raw", align_bytes=64)
+        ws3_raw = keep.tile([P, N], U8, name="ws3_raw", align_bytes=64)
+        nc.vector.memset(ws12_raw[:].bitcast(I32), 0)
+        nc.vector.memset(ws3_raw[:].bitcast(I32), 0)
+
+        def load_scales(queue, tile, first, scales):
+            for q in range(4):
+                queue.dma_start(tile[32 * q + first : 32 * q + first + 4, :].bitcast(I32), scales[0, 4 * q : 4 * q + 4, :].bitcast(I32))
+
+        for q in range(4):
+            rows = x_scales[0, 4 * q : 4 * q + 4, :].bitcast(I32)
+            nc.sync.dma_start(xs[32 * q : 32 * q + 32, :].bitcast(I32), rows.unsqueeze(0).to_broadcast([8, 4, T // 4]))
+        nc.sync.dma_start(offs_l[:], offs)
+        nc.sync.dma_start(two_l[:], two)
+        nc.sync.dma_start(xw[:], word_rows(x_words))
+        nc.sync.dma_start(w1_raw[:], word_rows(w1_words))
+        nc.gpsimd.dma_start(gain[:], gn.rearrange("(p t) o -> p (t o)", t=PACK))
+        load_scales(nc.gpsimd, ws12_raw, 0, w1_scales)
+        load_scales(nc.sync, ws12_raw, 4, w2_scales)
+        nc.sync.dma_start(w2_raw[:], word_rows(w2_words))
+        for k, taps in enumerate((t1, t2, t3)):
+            nc.sync.dma_start(tap_l[k][:], taps)
+        nc.sync.dma_start(w3_raw[:], word_rows(w3_words))
+        load_scales(nc.sync, ws3_raw, 0, w3_scales)
+        nc.sync.dma_start(slot_l[:], slot)
+        make_identity(nc, ident[:])
+
+        nc.scalar.activation(half_gain[:], gain[:], ACT.Copy, scale=0.5)
+
+        def deal_words(raw, name):
+            dealt = keep.tile([P, H], U32, name=name, align_bytes=64)
+            nc.scalar.copy(dealt[:].rearrange("p (t m) -> p m t", t=PACK), raw[:].bitcast(U32).rearrange("p (m t) -> p m t", t=PACK))
+            return dealt
+
+        w1_d = deal_words(w1_raw, "w1_d")
+        w2_d = deal_words(w2_raw, "w2_d")
+
+        xs_offs = keep.tile([P, S], U8, name="xs_offs", align_bytes=64)
+        xs_two = keep.tile([P, S], U8, name="xs_two", align_bytes=64)
+        xw_offs = keep.tile([P, S], U32, name="xw_offs", align_bytes=64)
+        xw_two_first = keep.tile([P, BLK], U32, name="xw_two_first", align_bytes=64)
+        nc.vector.tensor_copy(xs_offs[:], xs[:].indirect(offs_l[:]))
+        nc.vector.tensor_copy(xs_two[:], xs[:].indirect(two_l[:]))
+        nc.vector.tensor_copy(xw_offs[:], xw[:].bitcast(U32).indirect(offs_l[:]))
+        ws12_d = keep.tile([P, H], U8, name="ws12_d", align_bytes=64)
+        nc.vector.tensor_copy(ws12_d[:].rearrange("p (t m) -> p m t", t=PACK), ws12_raw[:].rearrange("p (m t) -> p m t", t=PACK))
+        nc.vector.tensor_copy(xw_two_first[:], xw[:].bitcast(U32).indirect(two_l[:, 0:COLS]))
+        xw_two_rest = keep.tile([P, S - BLK], U32, name="xw_two_rest", tag="ws12_raw", align_bytes=64)
+        nc.vector.tensor_copy(xw_two_rest[:], xw[:].bitcast(U32).indirect(two_l[:, COLS:]))
+
+        neg_c = {}
+
+        def points(b):
+            bank = psum.tile([P, PACK, BLK], F32, name="c_bank", tag="c_bank")
+            moving = xw_two_first[:] if b == 0 else xw_two_rest[:, (b - 1) * BLK : b * BLK]
+            for t in range(PACK):
+                cols = slice(t * P, (t + 1) * P)
+                nc.tensor.matmul_mx(bank[:, t, :], w2_d[:, cols].bitcast(FP8X4), ws12_d[4:P, cols], moving.bitcast(FP8X4), xs_two[:, b * BLK : (b + 1) * BLK], start=True, stop=True)
+            neg_c[b] = keep.tile([P, PACK, BLK], F32, name="neg_c%d" % b, tag="neg_c%d" % b, align_bytes=64)
+            nc.scalar.activation(neg_c[b][:], bank[:], ACT.Copy, scale=-1.0)
+
+        y = []
+        for t in range(PACK):
+            bank = psum.tile([P, S], F32, name="y_bank", tag="bank%d" % t)
+            cols = slice(t * P, (t + 1) * P)
+            nc.tensor.matmul_mx(bank[:], w1_d[:, cols].bitcast(FP8X4), ws12_d[:, cols], xw_offs[:].bitcast(FP8X4), xs_offs[:], start=True, stop=True)
+            y.append(keep.tile([P, S], F32, name="y%d" % t))
+            nc.scalar.copy(y[t][:], bank[:])
+            if t == 0:
+                points(0)
+
+        w3_d = keep.tile([P, N], U32, name="w3_d", align_bytes=64)
+        nc.vector.tensor_copy(w3_d[:].rearrange("p (t m) -> p m t", t=PACK), w3_raw[:].bitcast(U32).rearrange("p (m t) -> p m t", t=PACK))
+        ws3_d = keep.tile([P, N], U8, name="ws3_d", align_bytes=64)
+        nc.vector.tensor_copy(ws3_d[:].rearrange("p (t m) -> p m t", t=PACK), ws3_raw[:].rearrange("p (m t) -> p m t", t=PACK))
+
+        page = []
+        mem_rows = mem.rearrange("(p t) u -> p t u", t=PACK)
+        for t in range(PACK):
+            page.append(keep.tile([P, U], F32, name="page%d" % t, tag="page%d" % t, align_bytes=64))
+            nc.sync.dma_start(page[t][:], mem_rows[:, t, :])
+
+        fetched = {}
+        whole = {}
+        sums = {}
+        zq = {}
+        h_sb = {}
+        h_bank = {}
+        ring = ["bank0", "bank1", "bank2"]
+        spare = ["bank3", "bank4"]
+
+        def fetch(b, t):
+            if PACK * b + t < VECTOR_TRIOS:
+                if t == 0:
+                    whole[b] = keep.tile([P, PACK, TAPS, BLK], F32, name="fetched%d" % b, tag=V_AFTER[b], align_bytes=64)
+                g = whole[b][:, t]
+            else:
+                g = keep.tile([P, TAPS, BLK], F32, name="fetched%d_%d" % (b, t), tag=FETCH_AFTER[b, t], align_bytes=64)
+            fetched[b, t] = g
+            for k in range(TAPS):
+                window = y[t][:].indirect(tap_l[k][:, b * COLS : (b + 1) * COLS])
+                if PACK * b + t < VECTOR_TRIOS:
+                    nc.vector.tensor_tensor(g[:, k, :], window, neg_c[b][:, t, :], ALU.add)
+                else:
+                    nc.scalar.activation(g[:, k, :], window, ACT.Copy)
+
+        def shade(b, t):
+            ring.append(ring.pop(0))
+            bank = psum.tile([P, TAPS, P], F32, name="diff_bank", tag=ring[-1])
+            for k in range(TAPS):
+                if PACK * b + t < VECTOR_TRIOS:
+                    nc.tensor.transpose(bank[:, k, :], fetched[b, t][:, k, :], ident[:])
+                else:
+                    nc.tensor.matmul(bank[:, k, :], neg_c[b][:, t, :], ident[:], start=True, stop=False, is_transpose=True)
+                    nc.tensor.matmul(bank[:, k, :], fetched[b, t][:, k, :], ident[:], start=False, stop=True, is_transpose=True)
+            hidden = keep.tile([P, TAPS, P], F32, name="hidden%d_%d" % (b, t), tag="hidden%d_%d" % (b, t), align_bytes=64)
+            nc.scalar.activation(hidden[:], bank[:], ACT.Tanh, scale=-1.5)
+            if b not in sums:
+                sums[b] = psum.tile([P, PACK, BLK], F32, name="sum_bank", tag="sum_bank", bufs=2)
+            for k in range(TAPS):
+                nc.tensor.matmul(sums[b][:, t, :], hidden[:, k, :], ident[:], start=(k == 0), stop=(k == TAPS - 1), is_transpose=True)
+
+        def layer(b):
+            z = keep.tile([P, BLK, PACK], BF16, name="z%d" % b, tag="z%d" % b, align_bytes=64)
+            nc.vector.tensor_tensor(z[:], sums[b][:].rearrange("p t j -> p j t"), half_gain[:].unsqueeze(1).to_broadcast([P, BLK, PACK]), ALU.mult)
+            z_words = keep.tile([P, BLK], U32, name="z_words%d" % b, align_bytes=64)
+            z_scales = keep.tile([P, BLK], U8, name="z_scales%d" % b, align_bytes=64)
+            nc.vector.quantize_mx(z_words[:].bitcast(FP8X4), z_scales[:], z[:].rearrange("p j t -> p (j t)"))
+            zq[b] = (z_words, z_scales)
+
+        def layer_product(b):
+            z_words, z_scales = zq[b]
+            spare.append(ring.pop())
+            ring.append(spare.pop(0))
+            h_bank[b] = psum.tile([P, PACK, BLK], F32, name="h_bank", tag=spare[-1])
+            for t in range(PACK):
+                cols = slice(t * P, (t + 1) * P)
+                nc.tensor.matmul_mx(h_bank[b][:, t, :], w3_d[:, cols].bitcast(FP8X4), ws3_d[:, cols], z_words[:].bitcast(FP8X4), z_scales[:], start=True, stop=True)
+            if b < NBLK - 1:
+                h_sb[b] = keep.tile([P, PACK, BLK if b < NBLK - 2 else 2 * BLK], F32, name="h_sb%d" % b)
+                nc.scalar.copy(h_sb[b][:, :, 0:BLK], h_bank[b][:])
+            else:
+                nc.scalar.copy(h_sb[b - 1][:, :, BLK:], h_bank[b][:])
+
+        def put(b, t, n=1):
+            src = h_sb[b][:, t, 0 : n * BLK] if b < NBLK - 1 else h_sb[b - 1][:, t, BLK:]
+            nc.vector.tensor_copy(page[t][:].indirect(slot_l[:, b * COLS : (b + n) * COLS]), src)
+
+        points(1)
+        fetch(0, 0)
+        shade(0, 0)
+        fetch(0, 1)
+        shade(0, 1)
+        fetch(2, 2)
+        fetch(0, 2)
+        shade(0, 2)
+        fetch(0, 3)
+        shade(0, 3)
+        layer(0)
+        points(2)
+        fetch(2, 3)
+        fetch(1, 0)
+        shade(1, 0)
+        fetch(1, 1)
+        shade(1, 1)
+        fetch(3, 0)
+        fetch(1, 2)
+        shade(1, 2)
+        fetch(1, 3)
+        shade(1, 3)
+        layer(1)
+        layer_product(0)
+        fetch(2, 0)
+        fetch(2, 1)
+        points(3)
+        shade(2, 2)
+        fetch(3, 1)
+        shade(2, 3)
+        fetch(3, 2)
+        shade(2, 0)
+        fetch(3, 3)
+        shade(2, 1)
+        layer(2)
+        layer_product(1)
+        put(0, 0)
+        put(0, 1)
+        put(0, 2)
+        put(0, 3)
+        shade(3, 0)
+        shade(3, 1)
+        shade(3, 2)
+        shade(3, 3)
+        layer(3)
+        layer_product(2)
+        layer_product(3)
+        put(1, 0)
+        put(1, 1)
+        put(1, 2)
+        put(1, 3)
+        put(2, 0)
+        put(2, 1)
+
+        out_rows = out_0.rearrange("(p t) u -> p t u", t=PACK)
+        pairs = [keep.tile([P, 2, QW, 2], BF16, name="pairs%d" % q, align_bytes=64) for q in range(NQ)]
+        for t in range(PACK):
+            if t < 2:
+                put(NBLK - 1, t)
+            else:
+                put(NBLK - 2, t, 2)
+            nc.sync.dma_start(out_rows[:, t, :], page[t][:])
+            for q in range(NQ):
+                nc.scalar.copy(pairs[q][:, t // 2, :, t % 2], page[t][:, q * QW : (q + 1) * QW])
+
+        out_scales = keep.tile([P, U], U8, name="out_scales", align_bytes=64)
+        for q in range(NQ):
+            grouped = keep.tile([P, QW, PACK], BF16, name="grouped%d" % q, align_bytes=64)
+            nc.vector.tensor_copy(grouped[:].rearrange("p s t -> p (s t)").bitcast(F32).rearrange("p (s u) -> p s u", u=2), pairs[q][:].rearrange("p u s e -> p u (s e)").bitcast(F32).rearrange("p u s -> p s u"))
+            out_words = keep.tile([P, QW], U32, name="out_words%d" % q, align_bytes=64)
+            nc.vector.quantize_mx(out_words[:].bitcast(FP8X4), out_scales[:, q * QW : (q + 1) * QW], grouped[:].rearrange("p s t -> p (s t)"))
+            nc.sync.dma_start(word_rows(out_1)[:, q * QW : (q + 1) * QW], out_words[:].bitcast(I32))
+        for q in range(4):
+            queue = nc.sync if q % 2 == 0 else nc.scalar
+            queue.dma_start(out_2[0, 4 * q : 4 * q + 4, :].bitcast(I32), out_scales[32 * q : 32 * q + 4, :].bitcast(I32))

@@ -18,15 +18,12 @@ FLOPS = 2 * (K * H * S * 2 + H * N * S)
 
 P = 128
 PACK = 4
-BLK = 128
-NBLK = S // BLK
+HALF = S // 2
+COLS = HALF // 16
 TAPS = 3
-COLS = BLK // 16
 NQ = 4
 QW = U // NQ
-VECTOR_TRIOS = 10
-FETCH_AFTER = {(b, t): "f%d_%d" % (b, t) for b in range(4) for t in range(4)}
-V_AFTER = {0: "first", 1: "neg_c0", 2: "z0"}
+SCALAR_PARTS = 2
 
 
 def tile_picked_shadowpcf_none_po_kernel(tc, x_words, x_scales, w1_words, w1_scales, w2_words, w2_scales, gn, w3_words, w3_scales, mem, offs, two, t1, t2, t3, slot, out_0, out_1, out_2):
@@ -67,9 +64,9 @@ def tile_picked_shadowpcf_none_po_kernel(tc, x_words, x_scales, w1_words, w1_sca
             nc.sync.dma_start(xs[32 * q : 32 * q + 32, :].bitcast(I32), rows.unsqueeze(0).to_broadcast([8, 4, T // 4]))
         nc.sync.dma_start(offs_l[:], offs)
         nc.sync.dma_start(two_l[:], two)
+        nc.sync.dma_start(gain[:], gn.rearrange("(p t) o -> p (t o)", t=PACK))
         nc.sync.dma_start(xw[:], word_rows(x_words))
         nc.sync.dma_start(w1_raw[:], word_rows(w1_words))
-        nc.gpsimd.dma_start(gain[:], gn.rearrange("(p t) o -> p (t o)", t=PACK))
         load_scales(nc.gpsimd, ws12_raw, 0, w1_scales)
         load_scales(nc.sync, ws12_raw, 4, w2_scales)
         nc.sync.dma_start(w2_raw[:], word_rows(w2_words))
@@ -93,36 +90,44 @@ def tile_picked_shadowpcf_none_po_kernel(tc, x_words, x_scales, w1_words, w1_sca
         xs_offs = keep.tile([P, S], U8, name="xs_offs", align_bytes=64)
         xs_two = keep.tile([P, S], U8, name="xs_two", align_bytes=64)
         xw_offs = keep.tile([P, S], U32, name="xw_offs", align_bytes=64)
-        xw_two_first = keep.tile([P, BLK], U32, name="xw_two_first", align_bytes=64)
         nc.vector.tensor_copy(xs_offs[:], xs[:].indirect(offs_l[:]))
         nc.vector.tensor_copy(xs_two[:], xs[:].indirect(two_l[:]))
         nc.vector.tensor_copy(xw_offs[:], xw[:].bitcast(U32).indirect(offs_l[:]))
         ws12_d = keep.tile([P, H], U8, name="ws12_d", align_bytes=64)
         nc.vector.tensor_copy(ws12_d[:].rearrange("p (t m) -> p m t", t=PACK), ws12_raw[:].rearrange("p (m t) -> p m t", t=PACK))
-        nc.vector.tensor_copy(xw_two_first[:], xw[:].bitcast(U32).indirect(two_l[:, 0:COLS]))
-        xw_two_rest = keep.tile([P, S - BLK], U32, name="xw_two_rest", tag="ws12_raw", align_bytes=64)
-        nc.vector.tensor_copy(xw_two_rest[:], xw[:].bitcast(U32).indirect(two_l[:, COLS:]))
+        xw_two = keep.tile([P, S], U32, name="xw_two", tag="ws12_raw", align_bytes=64)
+        for half in range(2):
+            nc.vector.tensor_copy(xw_two[:, half * HALF : (half + 1) * HALF], xw[:].bitcast(U32).indirect(two_l[:, half * COLS : (half + 1) * COLS]))
 
-        neg_c = {}
+        gain_bank = psum.tile([P, PACK, P], F32, name="gain_bank", tag="b4")
+        for t in range(PACK):
+            nc.tensor.transpose(gain_bank[:, t, :], half_gain[:, t : t + 1].to_broadcast([P, P]), ident[:])
+        gain_row = keep.tile([P, 2, P, 2], F32, name="gain_row")
+        nc.scalar.copy(gain_row[:], gain_bank[:].rearrange("j (u e) p -> j u p e", e=2))
 
-        def points(b):
-            bank = psum.tile([P, PACK, BLK], F32, name="c_bank", tag="c_bank")
-            moving = xw_two_first[:] if b == 0 else xw_two_rest[:, (b - 1) * BLK : b * BLK]
-            for t in range(PACK):
-                cols = slice(t * P, (t + 1) * P)
-                nc.tensor.matmul_mx(bank[:, t, :], w2_d[:, cols].bitcast(FP8X4), ws12_d[4:P, cols], moving.bitcast(FP8X4), xs_two[:, b * BLK : (b + 1) * BLK], start=True, stop=True)
-            neg_c[b] = keep.tile([P, PACK, BLK], F32, name="neg_c%d" % b, tag="neg_c%d" % b, align_bytes=64)
-            nc.scalar.activation(neg_c[b][:], bank[:], ACT.Copy, scale=-1.0)
+        c_of = {}
+
+        def points(half, pair):
+            bank = psum.tile([P, 2, HALF], F32, name="c_bank", tag=("b5", "b6", "b5", "b7")[2 * half + pair])
+            for e in range(2):
+                cols = slice((2 * pair + e) * P, (2 * pair + e + 1) * P)
+                nc.tensor.matmul_mx(bank[:, e, :], w2_d[:, cols].bitcast(FP8X4), ws12_d[4:P, cols], xw_two[:, half * HALF : (half + 1) * HALF].bitcast(FP8X4), xs_two[:, half * HALF : (half + 1) * HALF], start=True, stop=True)
+            tile = bank
+            if (half, pair) != (1, 1):
+                tile = keep.tile([P, 2, HALF], F32, name="c%d_%d" % (half, pair), tag="c%d_%d" % (half, pair), align_bytes=64)
+                nc.scalar.copy(tile[:], bank[:])
+            for e in range(2):
+                c_of[half, 2 * pair + e] = tile[:, e, :]
 
         y = []
         for t in range(PACK):
-            bank = psum.tile([P, S], F32, name="y_bank", tag="bank%d" % t)
+            bank = psum.tile([P, S], F32, name="y_bank", tag="b%d" % t)
             cols = slice(t * P, (t + 1) * P)
             nc.tensor.matmul_mx(bank[:], w1_d[:, cols].bitcast(FP8X4), ws12_d[:, cols], xw_offs[:].bitcast(FP8X4), xs_offs[:], start=True, stop=True)
             y.append(keep.tile([P, S], F32, name="y%d" % t))
             nc.scalar.copy(y[t][:], bank[:])
             if t == 0:
-                points(0)
+                points(0, 0)
 
         w3_d = keep.tile([P, N], U32, name="w3_d", align_bytes=64)
         nc.vector.tensor_copy(w3_d[:].rearrange("p (t m) -> p m t", t=PACK), w3_raw[:].bitcast(U32).rearrange("p (m t) -> p m t", t=PACK))
@@ -135,144 +140,147 @@ def tile_picked_shadowpcf_none_po_kernel(tc, x_words, x_scales, w1_words, w1_sca
             page.append(keep.tile([P, U], F32, name="page%d" % t, tag="page%d" % t, align_bytes=64))
             nc.sync.dma_start(page[t][:], mem_rows[:, t, :])
 
-        fetched = {}
-        whole = {}
+        diff = {}
+        depth = {}
         sums = {}
         zq = {}
         h_sb = {}
-        h_bank = {}
-        ring = ["bank0", "bank1", "bank2"]
-        spare = ["bank3", "bank4"]
 
-        def fetch(b, t):
-            if PACK * b + t < VECTOR_TRIOS:
-                if t == 0:
-                    whole[b] = keep.tile([P, PACK, TAPS, BLK], F32, name="fetched%d" % b, tag=V_AFTER[b], align_bytes=64)
-                g = whole[b][:, t]
+        def sbuf(shape, dtype, name, after=None):
+            return keep.tile(shape, dtype, name=name, tag=after or name, align_bytes=64)
+
+        def window(half, t, k):
+            return y[t][:].indirect(tap_l[k][:, half * COLS : (half + 1) * COLS])
+
+        def fetch_diff(half, t, after=None):
+            diff[half, t] = sbuf([P, TAPS, HALF], F32, "diff%d_%d" % (half, t), after)
+            for k in range(TAPS):
+                nc.vector.tensor_tensor(diff[half, t][:, k, :], window(half, t, k), c_of[half, t], ALU.subtract)
+
+        def fetch_depth(half, t, k, after=None):
+            if k == 0:
+                depth[half, t] = sbuf([P, TAPS, HALF], F32, "depth%d_%d" % (half, t), after)
+            nc.scalar.activation(depth[half, t][:, k, :], window(half, t, k), ACT.Copy)
+
+        def subtract(half, t, after=None):
+            diff[half, t] = sbuf([P, TAPS, HALF], F32, "diff%d_%d" % (half, t), after)
+            nc.vector.tensor_tensor(diff[half, t][:], depth[half, t][:], c_of[half, t].unsqueeze(1).to_broadcast([P, TAPS, HALF]), ALU.subtract)
+
+        def shade(half, t):
+            hidden = sbuf([P, TAPS, HALF], F32, "hidden%d_%d" % (half, t))
+            nc.scalar.activation(hidden[:], diff[half, t][:], ACT.Tanh, scale=-1.5)
+            for j in range(2):
+                if (half, j) not in sums:
+                    sums[half, j] = psum.tile([P, PACK, P], F32, name="sum_bank", tag="b%d" % (2 * half + j))
+                for k in range(TAPS):
+                    nc.tensor.matmul(sums[half, j][:, t, :], hidden[:, k, j * P : (j + 1) * P], ident[:], start=(k == 0), stop=(k == TAPS - 1), is_transpose=True)
+
+        def layer(half):
+            z_turned = sbuf([P, 2, 2, P, 2], BF16, "z_turned%d" % half)
+            back = psum.tile([P, 2, 2, P], F32, name="back_bank", tag=("b4", "b5")[half])
+            for j in range(2):
+                nc.vector.tensor_tensor(z_turned[:, j], sums[half, j][:].rearrange("j (u e) p -> j u p e", e=2), gain_row[:], ALU.mult)
+                for u in range(2):
+                    nc.tensor.transpose(back[:, j, u, :], z_turned[:, j, u].rearrange("j p e -> j (p e)").bitcast(F32), ident[:])
+            z = sbuf([P, HALF * PACK], BF16, "z%d" % half)
+            nc.scalar.copy(z[:].bitcast(F32).rearrange("p (b j u) -> p b j u", b=2, u=2), back[:].rearrange("p b u j -> p b j u"))
+            z_words = sbuf([P, HALF], U32, "z_words%d" % half)
+            z_scales = sbuf([P, HALF], U8, "z_scales%d" % half)
+            nc.vector.quantize_mx(z_words[:].bitcast(FP8X4), z_scales[:], z[:])
+            zq[half] = (z_words, z_scales)
+
+        def layer_product(half, pair, after=(None, None)):
+            z_words, z_scales = zq[half]
+            bank = psum.tile([P, 2, HALF], F32, name="h_bank", tag=("b6", "b0", "b1", "b2")[2 * half + pair])
+            for e in range(2):
+                cols = slice((2 * pair + e) * P, (2 * pair + e + 1) * P)
+                nc.tensor.matmul_mx(bank[:, e, :], w3_d[:, cols].bitcast(FP8X4), ws3_d[:, cols], z_words[:].bitcast(FP8X4), z_scales[:], start=True, stop=True)
+            if after[0] is None:
+                tile = sbuf([P, 2, HALF], F32, "h%d_%d" % (half, pair))
+                nc.scalar.copy(tile[:], bank[:])
+                for e in range(2):
+                    h_sb[half, 2 * pair + e] = tile[:, e, :]
             else:
-                g = keep.tile([P, TAPS, BLK], F32, name="fetched%d_%d" % (b, t), tag=FETCH_AFTER[b, t], align_bytes=64)
-            fetched[b, t] = g
-            for k in range(TAPS):
-                window = y[t][:].indirect(tap_l[k][:, b * COLS : (b + 1) * COLS])
-                if PACK * b + t < VECTOR_TRIOS:
-                    nc.vector.tensor_tensor(g[:, k, :], window, neg_c[b][:, t, :], ALU.add)
-                else:
-                    nc.scalar.activation(g[:, k, :], window, ACT.Copy)
+                for e in range(2):
+                    tile = sbuf([P, HALF], F32, "h%d_%d_%d" % (half, pair, e), after[e])
+                    nc.scalar.copy(tile[:], bank[:, e, :])
+                    h_sb[half, 2 * pair + e] = tile[:]
 
-        def shade(b, t):
-            ring.append(ring.pop(0))
-            bank = psum.tile([P, TAPS, P], F32, name="diff_bank", tag=ring[-1])
-            for k in range(TAPS):
-                if PACK * b + t < VECTOR_TRIOS:
-                    nc.tensor.transpose(bank[:, k, :], fetched[b, t][:, k, :], ident[:])
-                else:
-                    nc.tensor.matmul(bank[:, k, :], neg_c[b][:, t, :], ident[:], start=True, stop=False, is_transpose=True)
-                    nc.tensor.matmul(bank[:, k, :], fetched[b, t][:, k, :], ident[:], start=False, stop=True, is_transpose=True)
-            hidden = keep.tile([P, TAPS, P], F32, name="hidden%d_%d" % (b, t), tag="hidden%d_%d" % (b, t), align_bytes=64)
-            nc.scalar.activation(hidden[:], bank[:], ACT.Tanh, scale=-1.5)
-            if b not in sums:
-                sums[b] = psum.tile([P, PACK, BLK], F32, name="sum_bank", tag="sum_bank", bufs=2)
-            for k in range(TAPS):
-                nc.tensor.matmul(sums[b][:, t, :], hidden[:, k, :], ident[:], start=(k == 0), stop=(k == TAPS - 1), is_transpose=True)
+        def put(half, t):
+            nc.vector.tensor_copy(page[t][:].indirect(slot_l[:, half * COLS : (half + 1) * COLS]), h_sb[half, t])
 
-        def layer(b):
-            z = keep.tile([P, BLK, PACK], BF16, name="z%d" % b, tag="z%d" % b, align_bytes=64)
-            nc.vector.tensor_tensor(z[:], sums[b][:].rearrange("p t j -> p j t"), half_gain[:].unsqueeze(1).to_broadcast([P, BLK, PACK]), ALU.mult)
-            z_words = keep.tile([P, BLK], U32, name="z_words%d" % b, align_bytes=64)
-            z_scales = keep.tile([P, BLK], U8, name="z_scales%d" % b, align_bytes=64)
-            nc.vector.quantize_mx(z_words[:].bitcast(FP8X4), z_scales[:], z[:].rearrange("p j t -> p (j t)"))
-            zq[b] = (z_words, z_scales)
-
-        def layer_product(b):
-            z_words, z_scales = zq[b]
-            spare.append(ring.pop())
-            ring.append(spare.pop(0))
-            h_bank[b] = psum.tile([P, PACK, BLK], F32, name="h_bank", tag=spare[-1])
-            for t in range(PACK):
-                cols = slice(t * P, (t + 1) * P)
-                nc.tensor.matmul_mx(h_bank[b][:, t, :], w3_d[:, cols].bitcast(FP8X4), ws3_d[:, cols], z_words[:].bitcast(FP8X4), z_scales[:], start=True, stop=True)
-            if b < NBLK - 1:
-                h_sb[b] = keep.tile([P, PACK, BLK if b < NBLK - 2 else 2 * BLK], F32, name="h_sb%d" % b)
-                nc.scalar.copy(h_sb[b][:, :, 0:BLK], h_bank[b][:])
-            else:
-                nc.scalar.copy(h_sb[b - 1][:, :, BLK:], h_bank[b][:])
-
-        def put(b, t, n=1):
-            src = h_sb[b][:, t, 0 : n * BLK] if b < NBLK - 1 else h_sb[b - 1][:, t, BLK:]
-            nc.vector.tensor_copy(page[t][:].indirect(slot_l[:, b * COLS : (b + n) * COLS]), src)
-
-        points(1)
-        fetch(0, 0)
+        points(0, 1)
+        points(1, 1)
+        fetch_diff(0, 0)
         shade(0, 0)
-        fetch(0, 1)
+        fetch_depth(0, 3, 0)
+        fetch_depth(0, 3, 1)
+        fetch_depth(0, 3, 2)
+        fetch_diff(0, 1)
         shade(0, 1)
-        fetch(2, 2)
-        fetch(0, 2)
+        points(1, 0)
+        fetch_diff(0, 2)
         shade(0, 2)
-        fetch(0, 3)
+        subtract(0, 3)
         shade(0, 3)
         layer(0)
-        points(2)
-        fetch(2, 3)
-        fetch(1, 0)
+        layer_product(0, 0)
+        fetch_depth(1, 3, 0)
+        fetch_depth(1, 3, 1)
+        fetch_depth(1, 3, 2)
+        fetch_depth(1, 2, 0, "z_turned0")
+        fetch_depth(1, 2, 1)
+        fetch_depth(1, 2, 2)
+        fetch_diff(1, 0, "c0_1")
+        fetch_diff(1, 1, "hidden0_3")
+        subtract(1, 3, "z0")
+        subtract(1, 2, "depth1_3")
         shade(1, 0)
-        fetch(1, 1)
         shade(1, 1)
-        fetch(3, 0)
-        fetch(1, 2)
-        shade(1, 2)
-        fetch(1, 3)
         shade(1, 3)
+        shade(1, 2)
         layer(1)
-        layer_product(0)
-        fetch(2, 0)
-        fetch(2, 1)
-        points(3)
-        shade(2, 2)
-        fetch(3, 1)
-        shade(2, 3)
-        fetch(3, 2)
-        shade(2, 0)
-        fetch(3, 3)
-        shade(2, 1)
-        layer(2)
-        layer_product(1)
+        layer_product(0, 1, ("hidden1_2", "z_turned1"))
+        layer_product(1, 0)
+        layer_product(1, 1)
         put(0, 0)
         put(0, 1)
         put(0, 2)
         put(0, 3)
-        shade(3, 0)
-        shade(3, 1)
-        shade(3, 2)
-        shade(3, 3)
-        layer(3)
-        layer_product(2)
-        layer_product(3)
-        put(1, 0)
-        put(1, 1)
-        put(1, 2)
-        put(1, 3)
-        put(2, 0)
-        put(2, 1)
 
         out_rows = out_0.rearrange("(p t) u -> p t u", t=PACK)
         pairs = [keep.tile([P, 2, QW, 2], BF16, name="pairs%d" % q, align_bytes=64) for q in range(NQ)]
+
+        def round_rows(copy, t, q):
+            copy(pairs[q][:, t // 2, :, t % 2], page[t][:, q * QW : (q + 1) * QW])
+
         for t in range(PACK):
-            if t < 2:
-                put(NBLK - 1, t)
-            else:
-                put(NBLK - 2, t, 2)
+            put(1, t)
             nc.sync.dma_start(out_rows[:, t, :], page[t][:])
-            for q in range(NQ):
-                nc.scalar.copy(pairs[q][:, t // 2, :, t % 2], page[t][:, q * QW : (q + 1) * QW])
+            for q in range(NQ if t < 2 else SCALAR_PARTS):
+                round_rows(nc.scalar.copy, t, q)
 
         out_scales = keep.tile([P, U], U8, name="out_scales", align_bytes=64)
-        for q in range(NQ):
-            grouped = keep.tile([P, QW, PACK], BF16, name="grouped%d" % q, align_bytes=64)
-            nc.vector.tensor_copy(grouped[:].rearrange("p s t -> p (s t)").bitcast(F32).rearrange("p (s u) -> p s u", u=2), pairs[q][:].rearrange("p u s e -> p u (s e)").bitcast(F32).rearrange("p u s -> p s u"))
+        grouped = {}
+
+        def weave(copy, q):
+            grouped[q] = keep.tile([P, QW * PACK], BF16, name="grouped%d" % q, align_bytes=64)
+            copy(grouped[q][:].bitcast(F32).rearrange("p (s u) -> p s u", u=2), pairs[q][:].rearrange("p u s e -> p u (s e)").bitcast(F32).rearrange("p u s -> p s u"))
+
+        def hand_on(q):
             out_words = keep.tile([P, QW], U32, name="out_words%d" % q, align_bytes=64)
-            nc.vector.quantize_mx(out_words[:].bitcast(FP8X4), out_scales[:, q * QW : (q + 1) * QW], grouped[:].rearrange("p s t -> p (s t)"))
+            nc.vector.quantize_mx(out_words[:].bitcast(FP8X4), out_scales[:, q * QW : (q + 1) * QW], grouped[q][:])
             nc.sync.dma_start(word_rows(out_1)[:, q * QW : (q + 1) * QW], out_words[:].bitcast(I32))
+
+        for q in range(SCALAR_PARTS):
+            weave(nc.scalar.copy, q)
+        for t in range(2, PACK):
+            for q in range(SCALAR_PARTS, NQ):
+                round_rows(nc.vector.tensor_copy, t, q)
+        for q in range(SCALAR_PARTS, NQ):
+            weave(nc.vector.tensor_copy, q)
+        for q in list(range(SCALAR_PARTS, NQ)) + list(range(SCALAR_PARTS)):
+            hand_on(q)
         for q in range(4):
             queue = nc.sync if q % 2 == 0 else nc.scalar
             queue.dma_start(out_2[0, 4 * q : 4 * q + 4, :].bitcast(I32), out_scales[32 * q : 32 * q + 4, :].bitcast(I32))

@@ -17,16 +17,19 @@ K, T, S, N, H, U = 512, 2048, 512, 512, 512, 1024
 FLOPS = 2 * (K * H * S * 2 + H * N * S)
 
 P = 128
-PACK = 4
+LANES = 4
+QUADRANTS = 4
 HALF = S // 2
 COLS = HALF // 16
 TAPS = 3
-NQ = 4
-QW = U // NQ
+PARTS = 4
+PART = U // PARTS
 SCALAR_PARTS = 2
 
 
-def tile_picked_shadowpcf_none_po_kernel(tc, x_words, x_scales, w1_words, w1_scales, w2_words, w2_scales, gn, w3_words, w3_scales, mem, offs, two, t1, t2, t3, slot, out_0, out_1, out_2):
+def tile_picked_shadowpcf_none_po_kernel(
+    tc, x_words, x_scales, w1_words, w1_scales, w2_words, w2_scales, gn, w3_words, w3_scales, mem, offs, two, t1, t2, t3, slot, out_0, out_1, out_2
+):
     nc = tc.nc
 
     def word_rows(words):
@@ -37,250 +40,260 @@ def tile_picked_shadowpcf_none_po_kernel(tc, x_words, x_scales, w1_words, w1_sca
         keep = ctx.enter_context(tc.tile_pool(name="keep", bufs=1))
         psum = ctx.enter_context(tc.psum_pool(name="psum", bufs=1))
 
-        offs_l = lists.tile([P, S // 16], U16, name="offs_l")
-        two_l = lists.tile([P, S // 16], U16, name="two_l")
-        tap_l = [lists.tile([P, S // 16], U16, name="tap_l%d" % k) for k in range(TAPS)]
-        slot_l = lists.tile([P, S // 16], U16, name="slot_l")
+        def sbuf(shape, dtype, name, after=None):
+            return keep.tile(shape, dtype, name=name, tag=after or name, align_bytes=64)
 
-        xs = keep.tile([P, T], U8, name="xs", tag="page3", align_bytes=64)
-        xw = keep.tile([P, T], I32, name="xw", tag="page0", align_bytes=64)
-        w1_raw = keep.tile([P, H], I32, name="w1_raw", tag="page1", align_bytes=64)
-        w2_raw = keep.tile([P, H], I32, name="w2_raw", tag="page2", align_bytes=64)
-        w3_raw = keep.tile([P, N], I32, name="w3_raw", align_bytes=64)
-        gain = keep.tile([P, PACK], F32, name="gain")
-        half_gain = keep.tile([P, PACK], F32, name="half_gain")
+        offs_list = lists.tile([P, S // 16], U16, name="offs_list")
+        two_list = lists.tile([P, S // 16], U16, name="two_list")
+        tap_list = [lists.tile([P, S // 16], U16, name="tap_list%d" % k) for k in range(TAPS)]
+        slot_list = lists.tile([P, S // 16], U16, name="slot_list")
+
+        table_bytes = sbuf([P, T], U8, "table_bytes", "page3")
+        table_words = sbuf([P, T], I32, "table_words", "page0")
+        w1_raw = sbuf([P, H], I32, "w1_raw", "page1")
+        w2_raw = sbuf([P, H], I32, "w2_raw", "page2")
+        w3_raw = sbuf([P, N], I32, "w3_raw")
+        gain = keep.tile([P, LANES], F32, name="gain")
+        half_gain = keep.tile([P, LANES], F32, name="half_gain")
         ident = keep.tile([P, P], F32, name="ident")
-        ws12_raw = keep.tile([P, H], U8, name="ws12_raw", tag="ws12_raw", align_bytes=64)
-        ws3_raw = keep.tile([P, N], U8, name="ws3_raw", align_bytes=64)
-        nc.vector.memset(ws12_raw[:].bitcast(I32), 0)
-        nc.vector.memset(ws3_raw[:].bitcast(I32), 0)
+        bytes_raw = [sbuf([P, H], U8, "bytes_raw%d" % i) for i in range(3)]
+        for tile in bytes_raw:
+            nc.vector.memset(tile[:].bitcast(I32), 0)
 
-        def load_scales(queue, tile, first, scales):
-            for q in range(4):
-                queue.dma_start(tile[32 * q + first : 32 * q + first + 4, :].bitcast(I32), scales[0, 4 * q : 4 * q + 4, :].bitcast(I32))
+        def load_scale_rows(tile, scales):
+            for q in range(QUADRANTS):
+                nc.sync.dma_start(tile[32 * q : 32 * q + 4, :].bitcast(I32), scales[0, 4 * q : 4 * q + 4, :].bitcast(I32))
 
-        for q in range(4):
+        nc.sync.dma_start(offs_list[:], offs)
+        for q in range(QUADRANTS):
             rows = x_scales[0, 4 * q : 4 * q + 4, :].bitcast(I32)
-            nc.sync.dma_start(xs[32 * q : 32 * q + 32, :].bitcast(I32), rows.unsqueeze(0).to_broadcast([8, 4, T // 4]))
-        nc.sync.dma_start(offs_l[:], offs)
-        nc.sync.dma_start(two_l[:], two)
-        nc.sync.dma_start(gain[:], gn.rearrange("(p t) o -> p (t o)", t=PACK))
-        nc.sync.dma_start(xw[:], word_rows(x_words))
+            nc.sync.dma_start(table_bytes[32 * q : 32 * q + 32, :].bitcast(I32), rows.unsqueeze(0).to_broadcast([8, 4, T // 4]))
+        nc.sync.dma_start(two_list[:], two)
+        nc.sync.dma_start(gain[:], gn.rearrange("(p t) o -> p (t o)", t=LANES))
+        nc.sync.dma_start(table_words[:], word_rows(x_words))
         nc.sync.dma_start(w1_raw[:], word_rows(w1_words))
-        load_scales(nc.gpsimd, ws12_raw, 0, w1_scales)
-        load_scales(nc.sync, ws12_raw, 4, w2_scales)
+        load_scale_rows(bytes_raw[0], w1_scales)
         nc.sync.dma_start(w2_raw[:], word_rows(w2_words))
+        load_scale_rows(bytes_raw[1], w2_scales)
         for k, taps in enumerate((t1, t2, t3)):
-            nc.sync.dma_start(tap_l[k][:], taps)
+            nc.sync.dma_start(tap_list[k][:], taps)
         nc.sync.dma_start(w3_raw[:], word_rows(w3_words))
-        load_scales(nc.sync, ws3_raw, 0, w3_scales)
-        nc.sync.dma_start(slot_l[:], slot)
+        load_scale_rows(bytes_raw[2], w3_scales)
+        nc.sync.dma_start(slot_list[:], slot)
         make_identity(nc, ident[:])
 
         nc.scalar.activation(half_gain[:], gain[:], ACT.Copy, scale=0.5)
 
-        def deal_words(raw, name):
-            dealt = keep.tile([P, H], U32, name=name, align_bytes=64)
-            nc.scalar.copy(dealt[:].rearrange("p (t m) -> p m t", t=PACK), raw[:].bitcast(U32).rearrange("p (m t) -> p m t", t=PACK))
+        def deal(copy, raw, dtype, name, after=None):
+            dealt = sbuf([P, H], dtype, name, after)
+            copy(dealt[:].rearrange("p (t m) -> p m t", t=LANES), raw.rearrange("p (m t) -> p m t", t=LANES))
             return dealt
 
-        w1_d = deal_words(w1_raw, "w1_d")
-        w2_d = deal_words(w2_raw, "w2_d")
+        w1_dealt = deal(nc.scalar.copy, w1_raw[:].bitcast(U32), U32, "w1_dealt")
+        w2_dealt = deal(nc.scalar.copy, w2_raw[:].bitcast(U32), U32, "w2_dealt")
 
-        xs_offs = keep.tile([P, S], U8, name="xs_offs", align_bytes=64)
-        xs_two = keep.tile([P, S], U8, name="xs_two", align_bytes=64)
-        xw_offs = keep.tile([P, S], U32, name="xw_offs", align_bytes=64)
-        nc.vector.tensor_copy(xs_offs[:], xs[:].indirect(offs_l[:]))
-        nc.vector.tensor_copy(xs_two[:], xs[:].indirect(two_l[:]))
-        nc.vector.tensor_copy(xw_offs[:], xw[:].bitcast(U32).indirect(offs_l[:]))
-        ws12_d = keep.tile([P, H], U8, name="ws12_d", align_bytes=64)
-        nc.vector.tensor_copy(ws12_d[:].rearrange("p (t m) -> p m t", t=PACK), ws12_raw[:].rearrange("p (m t) -> p m t", t=PACK))
-        xw_two = keep.tile([P, S], U32, name="xw_two", tag="ws12_raw", align_bytes=64)
+        texel_bytes = sbuf([P, S], U8, "texel_bytes")
+        point_bytes = sbuf([P, S], U8, "point_bytes")
+        texel_words = sbuf([P, S], U32, "texel_words")
+        nc.vector.tensor_copy(texel_bytes[:], table_bytes[:].indirect(offs_list[:]))
+        nc.vector.tensor_copy(point_bytes[:], table_bytes[:].indirect(two_list[:]))
+        nc.vector.tensor_copy(texel_words[:], table_words[:].bitcast(U32).indirect(offs_list[:]))
+        w1_bytes = deal(nc.vector.tensor_copy, bytes_raw[0][:], U8, "w1_bytes")
+        w2_bytes = deal(nc.vector.tensor_copy, bytes_raw[1][:], U8, "w2_bytes")
+        point_words = sbuf([P, S], U32, "point_words", "bytes_raw0")
         for half in range(2):
-            nc.vector.tensor_copy(xw_two[:, half * HALF : (half + 1) * HALF], xw[:].bitcast(U32).indirect(two_l[:, half * COLS : (half + 1) * COLS]))
+            nc.vector.tensor_copy(
+                point_words[:, half * HALF : (half + 1) * HALF],
+                table_words[:].bitcast(U32).indirect(two_list[:, half * COLS : (half + 1) * COLS]),
+            )
 
-        gain_bank = psum.tile([P, PACK, P], F32, name="gain_bank", tag="b4")
-        for t in range(PACK):
+        gain_bank = psum.tile([P, LANES, P], F32, name="gain_bank", tag="bank4")
+        for t in range(LANES):
             nc.tensor.transpose(gain_bank[:, t, :], half_gain[:, t : t + 1].to_broadcast([P, P]), ident[:])
         gain_row = keep.tile([P, 2, P, 2], F32, name="gain_row")
         nc.scalar.copy(gain_row[:], gain_bank[:].rearrange("j (u e) p -> j u p e", e=2))
 
-        c_of = {}
+        def product(out, words, scale_bytes, t, moving_words, moving_bytes):
+            places = slice(t * P, (t + 1) * P)
+            nc.tensor.matmul_mx(out, words[:, places].bitcast(FP8X4), scale_bytes[:, places], moving_words.bitcast(FP8X4), moving_bytes, start=True, stop=True)
 
-        def points(half, pair):
-            bank = psum.tile([P, 2, HALF], F32, name="c_bank", tag=("b5", "b6", "b5", "b7")[2 * half + pair])
+        c = {}
+
+        def points(half, pair, tag, fused_lanes):
+            bank = psum.tile([P, 2, HALF], F32, name="c_bank", tag=tag)
+            entries = slice(half * HALF, (half + 1) * HALF)
             for e in range(2):
-                cols = slice((2 * pair + e) * P, (2 * pair + e + 1) * P)
-                nc.tensor.matmul_mx(bank[:, e, :], w2_d[:, cols].bitcast(FP8X4), ws12_d[4:P, cols], xw_two[:, half * HALF : (half + 1) * HALF].bitcast(FP8X4), xs_two[:, half * HALF : (half + 1) * HALF], start=True, stop=True)
-            tile = bank
-            if (half, pair) != (1, 1):
-                tile = keep.tile([P, 2, HALF], F32, name="c%d_%d" % (half, pair), tag="c%d_%d" % (half, pair), align_bytes=64)
-                nc.scalar.copy(tile[:], bank[:])
-            for e in range(2):
-                c_of[half, 2 * pair + e] = tile[:, e, :]
+                product(bank[:, e, :], w2_dealt, w2_bytes, 2 * pair + e, point_words[:, entries], point_bytes[:, entries])
+                c[half, 2 * pair + e] = bank[:, e, :]
+            if fused_lanes:
+                first = fused_lanes[0] - 2 * pair
+                copied = sbuf([P, len(fused_lanes), HALF], F32, "c%d_%d" % (half, pair))
+                nc.scalar.copy(copied[:], bank[:, first : first + len(fused_lanes), :])
+                for i, t in enumerate(fused_lanes):
+                    c[half, t] = copied[:, i, :]
 
         y = []
-        for t in range(PACK):
-            bank = psum.tile([P, S], F32, name="y_bank", tag="b%d" % t)
-            cols = slice(t * P, (t + 1) * P)
-            nc.tensor.matmul_mx(bank[:], w1_d[:, cols].bitcast(FP8X4), ws12_d[:, cols], xw_offs[:].bitcast(FP8X4), xs_offs[:], start=True, stop=True)
+        for t in range(LANES):
+            bank = psum.tile([P, S], F32, name="y_bank", tag="bank%d" % t)
+            product(bank[:], w1_dealt, w1_bytes, t, texel_words[:], texel_bytes[:])
             y.append(keep.tile([P, S], F32, name="y%d" % t))
             nc.scalar.copy(y[t][:], bank[:])
-            if t == 0:
-                points(0, 0)
+        points(0, 0, "bank5", [1])
 
-        w3_d = keep.tile([P, N], U32, name="w3_d", align_bytes=64)
-        nc.vector.tensor_copy(w3_d[:].rearrange("p (t m) -> p m t", t=PACK), w3_raw[:].bitcast(U32).rearrange("p (m t) -> p m t", t=PACK))
-        ws3_d = keep.tile([P, N], U8, name="ws3_d", align_bytes=64)
-        nc.vector.tensor_copy(ws3_d[:].rearrange("p (t m) -> p m t", t=PACK), ws3_raw[:].rearrange("p (m t) -> p m t", t=PACK))
+        w3_bytes = deal(nc.vector.tensor_copy, bytes_raw[2][:], U8, "w3_bytes")
 
         page = []
-        mem_rows = mem.rearrange("(p t) u -> p t u", t=PACK)
-        for t in range(PACK):
-            page.append(keep.tile([P, U], F32, name="page%d" % t, tag="page%d" % t, align_bytes=64))
+        mem_rows = mem.rearrange("(p t) u -> p t u", t=LANES)
+        for t in range(LANES):
+            page.append(sbuf([P, U], F32, "page%d" % t))
             nc.sync.dma_start(page[t][:], mem_rows[:, t, :])
 
-        diff = {}
         depth = {}
+        diff = {}
         sums = {}
-        zq = {}
-        h_sb = {}
+        z_quantised = {}
+        h = {}
 
-        def sbuf(shape, dtype, name, after=None):
-            return keep.tile(shape, dtype, name=name, tag=after or name, align_bytes=64)
-
-        def window(half, t, k):
-            return y[t][:].indirect(tap_l[k][:, half * COLS : (half + 1) * COLS])
+        def tap_window(half, t, k):
+            return y[t][:].indirect(tap_list[k][:, half * COLS : (half + 1) * COLS])
 
         def fetch_diff(half, t, after=None):
             diff[half, t] = sbuf([P, TAPS, HALF], F32, "diff%d_%d" % (half, t), after)
             for k in range(TAPS):
-                nc.vector.tensor_tensor(diff[half, t][:, k, :], window(half, t, k), c_of[half, t], ALU.subtract)
+                nc.vector.tensor_tensor(diff[half, t][:, k, :], tap_window(half, t, k), c[half, t], ALU.subtract)
 
-        def fetch_depth(half, t, k, after=None):
-            if k == 0:
+        def fetch_depth_on_vector(half, t, taps):
+            depth[half, t] = sbuf([P, TAPS, HALF], F32, "depth%d_%d" % (half, t))
+            for k in taps:
+                nc.vector.tensor_copy(depth[half, t][:, k, :], tap_window(half, t, k))
+
+        def fetch_depth_on_scalar(half, t, taps=range(TAPS), after=None):
+            if (half, t) not in depth:
                 depth[half, t] = sbuf([P, TAPS, HALF], F32, "depth%d_%d" % (half, t), after)
-            nc.scalar.activation(depth[half, t][:, k, :], window(half, t, k), ACT.Copy)
+            for k in taps:
+                nc.scalar.activation(depth[half, t][:, k, :], tap_window(half, t, k), ACT.Copy)
 
         def subtract(half, t, after=None):
             diff[half, t] = sbuf([P, TAPS, HALF], F32, "diff%d_%d" % (half, t), after)
-            nc.vector.tensor_tensor(diff[half, t][:], depth[half, t][:], c_of[half, t].unsqueeze(1).to_broadcast([P, TAPS, HALF]), ALU.subtract)
+            nc.vector.tensor_tensor(diff[half, t][:], depth[half, t][:], c[half, t].unsqueeze(1).to_broadcast([P, TAPS, HALF]), ALU.subtract)
+
+        sum_tags = (("bank0", "bank1"), ("bank1", "bank4"))
 
         def shade(half, t):
             hidden = sbuf([P, TAPS, HALF], F32, "hidden%d_%d" % (half, t))
             nc.scalar.activation(hidden[:], diff[half, t][:], ACT.Tanh, scale=-1.5)
-            for j in range(2):
-                if (half, j) not in sums:
-                    sums[half, j] = psum.tile([P, PACK, P], F32, name="sum_bank", tag="b%d" % (2 * half + j))
+            for b in range(2):
+                if (half, b) not in sums:
+                    sums[half, b] = psum.tile([P, LANES, P], F32, name="sum_bank", tag=sum_tags[half][b])
                 for k in range(TAPS):
-                    nc.tensor.matmul(sums[half, j][:, t, :], hidden[:, k, j * P : (j + 1) * P], ident[:], start=(k == 0), stop=(k == TAPS - 1), is_transpose=True)
+                    nc.tensor.matmul(sums[half, b][:, t, :], hidden[:, k, b * P : (b + 1) * P], ident[:], start=(k == 0), stop=(k == TAPS - 1), is_transpose=True)
 
-        def layer(half):
-            z_turned = sbuf([P, 2, 2, P, 2], BF16, "z_turned%d" % half)
-            back = psum.tile([P, 2, 2, P], F32, name="back_bank", tag=("b4", "b5")[half])
-            for j in range(2):
-                nc.vector.tensor_tensor(z_turned[:, j], sums[half, j][:].rearrange("j (u e) p -> j u p e", e=2), gain_row[:], ALU.mult)
+        def quantise_z(half, tag):
+            back = psum.tile([P, 2, 2, P], F32, name="back_bank", tag=tag)
+            for b in range(2):
+                z_turned = sbuf([P, 2, P, 2], BF16, "z_turned%d_%d" % (half, b))
+                nc.vector.tensor_tensor(z_turned[:], sums[half, b][:].rearrange("j (u e) p -> j u p e", e=2), gain_row[:], ALU.mult)
                 for u in range(2):
-                    nc.tensor.transpose(back[:, j, u, :], z_turned[:, j, u].rearrange("j p e -> j (p e)").bitcast(F32), ident[:])
-            z = sbuf([P, HALF * PACK], BF16, "z%d" % half)
+                    nc.tensor.transpose(back[:, b, u, :], z_turned[:, u].rearrange("j p e -> j (p e)").bitcast(F32), ident[:])
+            z = sbuf([P, HALF * LANES], BF16, "z%d" % half)
             nc.scalar.copy(z[:].bitcast(F32).rearrange("p (b j u) -> p b j u", b=2, u=2), back[:].rearrange("p b u j -> p b j u"))
             z_words = sbuf([P, HALF], U32, "z_words%d" % half)
-            z_scales = sbuf([P, HALF], U8, "z_scales%d" % half)
-            nc.vector.quantize_mx(z_words[:].bitcast(FP8X4), z_scales[:], z[:])
-            zq[half] = (z_words, z_scales)
+            z_bytes = sbuf([P, HALF], U8, "z_bytes%d" % half)
+            nc.vector.quantize_mx(z_words[:].bitcast(FP8X4), z_bytes[:], z[:])
+            z_quantised[half] = (z_words, z_bytes)
 
-        def layer_product(half, pair, after=(None, None)):
-            z_words, z_scales = zq[half]
-            bank = psum.tile([P, 2, HALF], F32, name="h_bank", tag=("b6", "b0", "b1", "b2")[2 * half + pair])
+        def layer(half, pair, tag):
+            z_words, z_bytes = z_quantised[half]
+            bank = psum.tile([P, 2, HALF], F32, name="h_bank", tag=tag)
             for e in range(2):
-                cols = slice((2 * pair + e) * P, (2 * pair + e + 1) * P)
-                nc.tensor.matmul_mx(bank[:, e, :], w3_d[:, cols].bitcast(FP8X4), ws3_d[:, cols], z_words[:].bitcast(FP8X4), z_scales[:], start=True, stop=True)
-            if after[0] is None:
-                tile = sbuf([P, 2, HALF], F32, "h%d_%d" % (half, pair))
-                nc.scalar.copy(tile[:], bank[:])
-                for e in range(2):
-                    h_sb[half, 2 * pair + e] = tile[:, e, :]
-            else:
-                for e in range(2):
-                    tile = sbuf([P, HALF], F32, "h%d_%d_%d" % (half, pair, e), after[e])
-                    nc.scalar.copy(tile[:], bank[:, e, :])
-                    h_sb[half, 2 * pair + e] = tile[:]
+                product(bank[:, e, :], w3_dealt, w3_bytes, 2 * pair + e, z_words[:], z_bytes[:])
+            return bank
+
+        def leave_bank(half, first, source, after=None):
+            count = source.shape[1]
+            tile = sbuf([P, count, HALF], F32, "h%d_%d" % (half, first), after)
+            nc.scalar.copy(tile[:], source)
+            for i in range(count):
+                h[half, first + i] = tile[:, i, :]
 
         def put(half, t):
-            nc.vector.tensor_copy(page[t][:].indirect(slot_l[:, half * COLS : (half + 1) * COLS]), h_sb[half, t])
+            nc.vector.tensor_copy(page[t][:].indirect(slot_list[:, half * COLS : (half + 1) * COLS]), h[half, t])
 
-        points(0, 1)
-        points(1, 1)
-        fetch_diff(0, 0)
+        points(0, 1, "bank6", [2])
+        points(1, 1, "bank7", [])
+        fetch_depth_on_vector(0, 0, [0, 1])
+        fetch_depth_on_scalar(0, 0, [2])
+        subtract(0, 0)
+        fetch_depth_on_scalar(0, 3, [0])
         shade(0, 0)
-        fetch_depth(0, 3, 0)
-        fetch_depth(0, 3, 1)
-        fetch_depth(0, 3, 2)
+        fetch_depth_on_scalar(0, 3, [1, 2])
         fetch_diff(0, 1)
         shade(0, 1)
-        points(1, 0)
+        points(1, 0, "bank5", [0, 1])
         fetch_diff(0, 2)
         shade(0, 2)
         subtract(0, 3)
         shade(0, 3)
-        layer(0)
-        layer_product(0, 0)
-        fetch_depth(1, 3, 0)
-        fetch_depth(1, 3, 1)
-        fetch_depth(1, 3, 2)
-        fetch_depth(1, 2, 0, "z_turned0")
-        fetch_depth(1, 2, 1)
-        fetch_depth(1, 2, 2)
-        fetch_diff(1, 0, "c0_1")
-        fetch_diff(1, 1, "hidden0_3")
-        subtract(1, 3, "z0")
-        subtract(1, 2, "depth1_3")
-        shade(1, 0)
-        shade(1, 1)
-        shade(1, 3)
-        shade(1, 2)
-        layer(1)
-        layer_product(0, 1, ("hidden1_2", "z_turned1"))
-        layer_product(1, 0)
-        layer_product(1, 1)
-        put(0, 0)
-        put(0, 1)
-        put(0, 2)
-        put(0, 3)
+        quantise_z(0, "bank4")
+        w3_dealt = deal(nc.vector.tensor_copy, w3_raw[:].bitcast(U32), U32, "w3_dealt", "z_turned0_0")
+        leave_bank(0, 0, layer(0, 0, "bank6")[:])
 
-        out_rows = out_0.rearrange("(p t) u -> p t u", t=PACK)
-        pairs = [keep.tile([P, 2, QW, 2], BF16, name="pairs%d" % q, align_bytes=64) for q in range(NQ)]
+        fetch_depth_on_scalar(1, 3, after="diff0_2")
+        fetch_depth_on_scalar(1, 2, after="z_turned0_1")
+        fetch_diff(1, 0, "depth0_3")
+        subtract(1, 3, "hidden0_3")
+        fetch_diff(1, 1, "z0")
+        subtract(1, 2, "depth1_3")
+        for t in (0, 3, 1, 2):
+            shade(1, t)
+        quantise_z(1, "bank5")
+
+        late_bank = layer(0, 1, "bank2")
+        leave_bank(0, 2, late_bank[:, 0:1, :], "hidden1_2")
+        leave_bank(0, 3, late_bank[:, 1:2, :], "z_turned1_1")
+        leave_bank(1, 0, layer(1, 0, "bank0")[:])
+        leave_bank(1, 2, layer(1, 1, "bank3")[:])
+        for t in range(LANES):
+            put(0, t)
+
+        out_rows = out_0.rearrange("(p t) u -> p t u", t=LANES)
+        pairs = [sbuf([P, 2, PART, 2], BF16, "pairs%d" % q) for q in range(PARTS)]
 
         def round_rows(copy, t, q):
-            copy(pairs[q][:, t // 2, :, t % 2], page[t][:, q * QW : (q + 1) * QW])
+            copy(pairs[q][:, t // 2, :, t % 2], page[t][:, q * PART : (q + 1) * PART])
 
-        for t in range(PACK):
+        for t in range(LANES):
             put(1, t)
             nc.sync.dma_start(out_rows[:, t, :], page[t][:])
-            for q in range(NQ if t < 2 else SCALAR_PARTS):
+            for q in range(PARTS if t < 2 else SCALAR_PARTS):
                 round_rows(nc.scalar.copy, t, q)
 
-        out_scales = keep.tile([P, U], U8, name="out_scales", align_bytes=64)
-        grouped = {}
+        out_bytes = sbuf([P, U], U8, "out_bytes")
+        woven = {}
 
         def weave(copy, q):
-            grouped[q] = keep.tile([P, QW * PACK], BF16, name="grouped%d" % q, align_bytes=64)
-            copy(grouped[q][:].bitcast(F32).rearrange("p (s u) -> p s u", u=2), pairs[q][:].rearrange("p u s e -> p u (s e)").bitcast(F32).rearrange("p u s -> p s u"))
+            woven[q] = sbuf([P, PART * LANES], BF16, "woven%d" % q)
+            copy(
+                woven[q][:].bitcast(F32).rearrange("p (s u) -> p s u", u=2),
+                pairs[q][:].rearrange("p u s e -> p u (s e)").bitcast(F32).rearrange("p u s -> p s u"),
+            )
 
         def hand_on(q):
-            out_words = keep.tile([P, QW], U32, name="out_words%d" % q, align_bytes=64)
-            nc.vector.quantize_mx(out_words[:].bitcast(FP8X4), out_scales[:, q * QW : (q + 1) * QW], grouped[q][:])
-            nc.sync.dma_start(word_rows(out_1)[:, q * QW : (q + 1) * QW], out_words[:].bitcast(I32))
+            out_words = sbuf([P, PART], U32, "out_words%d" % q)
+            nc.vector.quantize_mx(out_words[:].bitcast(FP8X4), out_bytes[:, q * PART : (q + 1) * PART], woven[q][:])
+            nc.sync.dma_start(word_rows(out_1)[:, q * PART : (q + 1) * PART], out_words[:].bitcast(I32))
 
-        for q in range(SCALAR_PARTS):
+        scalar_parts = list(range(SCALAR_PARTS))
+        vector_parts = list(range(SCALAR_PARTS, PARTS))
+        for q in scalar_parts:
             weave(nc.scalar.copy, q)
-        for t in range(2, PACK):
-            for q in range(SCALAR_PARTS, NQ):
+        for t in range(2, LANES):
+            for q in vector_parts:
                 round_rows(nc.vector.tensor_copy, t, q)
-        for q in range(SCALAR_PARTS, NQ):
+        for q in vector_parts:
             weave(nc.vector.tensor_copy, q)
-        for q in list(range(SCALAR_PARTS, NQ)) + list(range(SCALAR_PARTS)):
+        for q in vector_parts + scalar_parts:
             hand_on(q)
-        for q in range(4):
+        for q in range(QUADRANTS):
             queue = nc.sync if q % 2 == 0 else nc.scalar
-            queue.dma_start(out_2[0, 4 * q : 4 * q + 4, :].bitcast(I32), out_scales[32 * q : 32 * q + 4, :].bitcast(I32))
+            queue.dma_start(out_2[0, 4 * q : 4 * q + 4, :].bitcast(I32), out_bytes[32 * q : 32 * q + 4, :].bitcast(I32))

@@ -60,9 +60,9 @@ def tile_picked_shadowpcf_none_po_kernel(
         for tile in bytes_raw:
             nc.vector.memset(tile[:].bitcast(I32), 0)
 
-        def load_scale_rows(tile, scales):
+        def load_scale_rows(queue, tile, scales):
             for q in range(QUADRANTS):
-                nc.sync.dma_start(tile[32 * q : 32 * q + 4, :].bitcast(I32), scales[0, 4 * q : 4 * q + 4, :].bitcast(I32))
+                queue.dma_start(tile[32 * q : 32 * q + 4, :].bitcast(I32), scales[0, 4 * q : 4 * q + 4, :].bitcast(I32))
 
         nc.sync.dma_start(offs_list[:], offs)
         for q in range(QUADRANTS):
@@ -72,13 +72,13 @@ def tile_picked_shadowpcf_none_po_kernel(
         nc.sync.dma_start(gain[:], gn.rearrange("(p t) o -> p (t o)", t=LANES))
         nc.sync.dma_start(table_words[:], word_rows(x_words))
         nc.sync.dma_start(w1_raw[:], word_rows(w1_words))
-        load_scale_rows(bytes_raw[0], w1_scales)
+        load_scale_rows(nc.sync, bytes_raw[0], w1_scales)
         nc.sync.dma_start(w2_raw[:], word_rows(w2_words))
-        load_scale_rows(bytes_raw[1], w2_scales)
+        load_scale_rows(nc.gpsimd, bytes_raw[1], w2_scales)
         for k, taps in enumerate((t1, t2, t3)):
             nc.sync.dma_start(tap_list[k][:], taps)
         nc.sync.dma_start(w3_raw[:], word_rows(w3_words))
-        load_scale_rows(bytes_raw[2], w3_scales)
+        load_scale_rows(nc.sync, bytes_raw[2], w3_scales)
         nc.sync.dma_start(slot_list[:], slot)
         make_identity(nc, ident[:])
 

from contextlib import ExitStack

import concourse.mybir as mybir
from concourse.masks import make_identity

F32 = mybir.dt.float32
BF16 = mybir.dt.bfloat16
U32 = mybir.dt.uint32
I32 = mybir.dt.int32
U16 = mybir.dt.uint16
U8 = mybir.dt.uint8
FP8X4 = mybir.dt.float8_e4m3fn_x4
ACT = mybir.ActivationFunctionType
ALU = mybir.AluOpType

K, T, S, N, H, U = 512, 2048, 512, 512, 512, 1024
FLOPS = 2 * (K * H * S * 2 + H * N * S)

P = 128
LANES = 4
QUADRANTS = 4
HALF = S // 2
COLS = HALF // 16
TAPS = 3
PARTS = 4
PART = U // PARTS
SCALAR_PARTS = 2


def tile_picked_shadowpcf_none_po_kernel(
    tc, x_words, x_scales, w1_words, w1_scales, w2_words, w2_scales, gn, w3_words, w3_scales, mem, offs, two, t1, t2, t3, slot, out_0, out_1, out_2
):
    nc = tc.nc

    def word_rows(words):
        return words[0].rearrange("p n r -> p (n r)").bitcast(I32)

    with ExitStack() as ctx:
        lists = ctx.enter_context(tc.tile_pool(name="lists", bufs=1))
        keep = ctx.enter_context(tc.tile_pool(name="keep", bufs=1))
        psum = ctx.enter_context(tc.psum_pool(name="psum", bufs=1))

        def sbuf(shape, dtype, name, after=None):
            return keep.tile(shape, dtype, name=name, tag=after or name, align_bytes=64)

        offs_list = lists.tile([P, S // 16], U16, name="offs_list")
        two_list = lists.tile([P, S // 16], U16, name="two_list")
        tap_list = [lists.tile([P, S // 16], U16, name="tap_list%d" % k) for k in range(TAPS)]
        slot_list = lists.tile([P, S // 16], U16, name="slot_list")

        table_bytes = sbuf([P, T], U8, "table_bytes", "page3")
        table_words = sbuf([P, T], I32, "table_words", "page0")
        w1_raw = sbuf([P, H], I32, "w1_raw", "page1")
        w2_raw = sbuf([P, H], I32, "w2_raw", "page2")
        w3_raw = sbuf([P, N], I32, "w3_raw")
        gain = keep.tile([P, LANES], F32, name="gain")
        half_gain = keep.tile([P, LANES], F32, name="half_gain")
        ident = keep.tile([P, P], F32, name="ident")
        bytes_raw = [sbuf([P, H], U8, "bytes_raw%d" % i) for i in range(3)]
        for tile in bytes_raw:
            nc.vector.memset(tile[:].bitcast(I32), 0)

        def load_scale_rows(queue, tile, scales):
            for q in range(QUADRANTS):
                queue.dma_start(tile[32 * q : 32 * q + 4, :].bitcast(I32), scales[0, 4 * q : 4 * q + 4, :].bitcast(I32))

        nc.sync.dma_start(offs_list[:], offs)
        for q in range(QUADRANTS):
            rows = x_scales[0, 4 * q : 4 * q + 4, :].bitcast(I32)
            nc.sync.dma_start(table_bytes[32 * q : 32 * q + 32, :].bitcast(I32), rows.unsqueeze(0).to_broadcast([8, 4, T // 4]))
        nc.sync.dma_start(two_list[:], two)
        nc.sync.dma_start(gain[:], gn.rearrange("(p t) o -> p (t o)", t=LANES))
        nc.sync.dma_start(table_words[:], word_rows(x_words))
        nc.sync.dma_start(w1_raw[:], word_rows(w1_words))
        load_scale_rows(nc.sync, bytes_raw[0], w1_scales)
        nc.sync.dma_start(w2_raw[:], word_rows(w2_words))
        load_scale_rows(nc.gpsimd, bytes_raw[1], w2_scales)
        for k, taps in enumerate((t1, t2, t3)):
            nc.sync.dma_start(tap_list[k][:], taps)
        nc.sync.dma_start(w3_raw[:], word_rows(w3_words))
        load_scale_rows(nc.sync, bytes_raw[2], w3_scales)
        nc.sync.dma_start(slot_list[:], slot)
        make_identity(nc, ident[:])

        nc.scalar.activation(half_gain[:], gain[:], ACT.Copy, scale=0.5)

        def deal(copy, raw, dtype, name, after=None):
            dealt = sbuf([P, H], dtype, name, after)
            copy(dealt[:].rearrange("p (t m) -> p m t", t=LANES), raw.rearrange("p (m t) -> p m t", t=LANES))
            return dealt

        w1_dealt = deal(nc.scalar.copy, w1_raw[:].bitcast(U32), U32, "w1_dealt")
        w2_dealt = deal(nc.scalar.copy, w2_raw[:].bitcast(U32), U32, "w2_dealt")

        texel_bytes = sbuf([P, S], U8, "texel_bytes")
        point_bytes = sbuf([P, S], U8, "point_bytes")
        texel_words = sbuf([P, S], U32, "texel_words")
        nc.vector.tensor_copy(texel_bytes[:], table_bytes[:].indirect(offs_list[:]))
        nc.vector.tensor_copy(point_bytes[:], table_bytes[:].indirect(two_list[:]))
        nc.vector.tensor_copy(texel_words[:], table_words[:].bitcast(U32).indirect(offs_list[:]))
        w1_bytes = deal(nc.vector.tensor_copy, bytes_raw[0][:], U8, "w1_bytes")
        w2_bytes = deal(nc.vector.tensor_copy, bytes_raw[1][:], U8, "w2_bytes")
        point_words = sbuf([P, S], U32, "point_words", "bytes_raw0")
        for half in range(2):
            nc.vector.tensor_copy(
                point_words[:, half * HALF : (half + 1) * HALF],
                table_words[:].bitcast(U32).indirect(two_list[:, half * COLS : (half + 1) * COLS]),
            )

        gain_bank = psum.tile([P, LANES, P], F32, name="gain_bank", tag="bank4")
        for t in range(LANES):
            nc.tensor.transpose(gain_bank[:, t, :], half_gain[:, t : t + 1].to_broadcast([P, P]), ident[:])
        gain_row = keep.tile([P, 2, P, 2], F32, name="gain_row")
        nc.scalar.copy(gain_row[:], gain_bank[:].rearrange("j (u e) p -> j u p e", e=2))

        def product(out, words, scale_bytes, t, moving_words, moving_bytes):
            places = slice(t * P, (t + 1) * P)
            nc.tensor.matmul_mx(out, words[:, places].bitcast(FP8X4), scale_bytes[:, places], moving_words.bitcast(FP8X4), moving_bytes, start=True, stop=True)

        c = {}

        def points(half, pair, tag, fused_lanes):
            bank = psum.tile([P, 2, HALF], F32, name="c_bank", tag=tag)
            entries = slice(half * HALF, (half + 1) * HALF)
            for e in range(2):
                product(bank[:, e, :], w2_dealt, w2_bytes, 2 * pair + e, point_words[:, entries], point_bytes[:, entries])
                c[half, 2 * pair + e] = bank[:, e, :]
            if fused_lanes:
                first = fused_lanes[0] - 2 * pair
                copied = sbuf([P, len(fused_lanes), HALF], F32, "c%d_%d" % (half, pair))
                nc.scalar.copy(copied[:], bank[:, first : first + len(fused_lanes), :])
                for i, t in enumerate(fused_lanes):
                    c[half, t] = copied[:, i, :]

        y = []
        for t in range(LANES):
            bank = psum.tile([P, S], F32, name="y_bank", tag="bank%d" % t)
            product(bank[:], w1_dealt, w1_bytes, t, texel_words[:], texel_bytes[:])
            y.append(keep.tile([P, S], F32, name="y%d" % t))
            nc.scalar.copy(y[t][:], bank[:])
        points(0, 0, "bank5", [1])

        w3_bytes = deal(nc.vector.tensor_copy, bytes_raw[2][:], U8, "w3_bytes")

        page = []
        mem_rows = mem.rearrange("(p t) u -> p t u", t=LANES)
        for t in range(LANES):
            page.append(sbuf([P, U], F32, "page%d" % t))
            nc.sync.dma_start(page[t][:], mem_rows[:, t, :])

        depth = {}
        diff = {}
        sums = {}
        z_quantised = {}
        h = {}

        def tap_window(half, t, k):
            return y[t][:].indirect(tap_list[k][:, half * COLS : (half + 1) * COLS])

        def fetch_diff(half, t, after=None):
            diff[half, t] = sbuf([P, TAPS, HALF], F32, "diff%d_%d" % (half, t), after)
            for k in range(TAPS):
                nc.vector.tensor_tensor(diff[half, t][:, k, :], tap_window(half, t, k), c[half, t], ALU.subtract)

        def fetch_depth_on_vector(half, t, taps):
            depth[half, t] = sbuf([P, TAPS, HALF], F32, "depth%d_%d" % (half, t))
            for k in taps:
                nc.vector.tensor_copy(depth[half, t][:, k, :], tap_window(half, t, k))

        def fetch_depth_on_scalar(half, t, taps=range(TAPS), after=None):
            if (half, t) not in depth:
                depth[half, t] = sbuf([P, TAPS, HALF], F32, "depth%d_%d" % (half, t), after)
            for k in taps:
                nc.scalar.activation(depth[half, t][:, k, :], tap_window(half, t, k), ACT.Copy)

        def subtract(half, t, after=None):
            diff[half, t] = sbuf([P, TAPS, HALF], F32, "diff%d_%d" % (half, t), after)
            nc.vector.tensor_tensor(diff[half, t][:], depth[half, t][:], c[half, t].unsqueeze(1).to_broadcast([P, TAPS, HALF]), ALU.subtract)

        sum_tags = (("bank0", "bank1"), ("bank1", "bank4"))

        def shade(half, t):
            hidden = sbuf([P, TAPS, HALF], F32, "hidden%d_%d" % (half, t))
            nc.scalar.activation(hidden[:], diff[half, t][:], ACT.Tanh, scale=-1.5)
            for b in range(2):
                if (half, b) not in sums:
                    sums[half, b] = psum.tile([P, LANES, P], F32, name="sum_bank", tag=sum_tags[half][b])
                for k in range(TAPS):
                    nc.tensor.matmul(sums[half, b][:, t, :], hidden[:, k, b * P : (b + 1) * P], ident[:], start=(k == 0), stop=(k == TAPS - 1), is_transpose=True)

        def quantise_z(half, tag):
            back = psum.tile([P, 2, 2, P], F32, name="back_bank", tag=tag)
            for b in range(2):
                z_turned = sbuf([P, 2, P, 2], BF16, "z_turned%d_%d" % (half, b))
                nc.vector.tensor_tensor(z_turned[:], sums[half, b][:].rearrange("j (u e) p -> j u p e", e=2), gain_row[:], ALU.mult)
                for u in range(2):
                    nc.tensor.transpose(back[:, b, u, :], z_turned[:, u].rearrange("j p e -> j (p e)").bitcast(F32), ident[:])
            z = sbuf([P, HALF * LANES], BF16, "z%d" % half)
            nc.scalar.copy(z[:].bitcast(F32).rearrange("p (b j u) -> p b j u", b=2, u=2), back[:].rearrange("p b u j -> p b j u"))
            z_words = sbuf([P, HALF], U32, "z_words%d" % half)
            z_bytes = sbuf([P, HALF], U8, "z_bytes%d" % half)
            nc.vector.quantize_mx(z_words[:].bitcast(FP8X4), z_bytes[:], z[:])
            z_quantised[half] = (z_words, z_bytes)

        def layer(half, pair, tag):
            z_words, z_bytes = z_quantised[half]
            bank = psum.tile([P, 2, HALF], F32, name="h_bank", tag=tag)
            for e in range(2):
                product(bank[:, e, :], w3_dealt, w3_bytes, 2 * pair + e, z_words[:], z_bytes[:])
            return bank

        def leave_bank(half, first, source, after=None):
            count = source.shape[1]
            tile = sbuf([P, count, HALF], F32, "h%d_%d" % (half, first), after)
            nc.scalar.copy(tile[:], source)
            for i in range(count):
                h[half, first + i] = tile[:, i, :]

        def put(half, t):
            nc.vector.tensor_copy(page[t][:].indirect(slot_list[:, half * COLS : (half + 1) * COLS]), h[half, t])

        points(0, 1, "bank6", [2])
        points(1, 1, "bank7", [])
        fetch_depth_on_vector(0, 0, [0, 1])
        fetch_depth_on_scalar(0, 0, [2])
        subtract(0, 0)
        fetch_depth_on_scalar(0, 3, [0])
        shade(0, 0)
        fetch_depth_on_scalar(0, 3, [1, 2])
        fetch_diff(0, 1)
        shade(0, 1)
        points(1, 0, "bank5", [0, 1])
        fetch_diff(0, 2)
        shade(0, 2)
        subtract(0, 3)
        shade(0, 3)
        quantise_z(0, "bank4")
        w3_dealt = deal(nc.vector.tensor_copy, w3_raw[:].bitcast(U32), U32, "w3_dealt", "z_turned0_0")
        leave_bank(0, 0, layer(0, 0, "bank6")[:])

        fetch_depth_on_scalar(1, 3, after="diff0_2")
        fetch_depth_on_scalar(1, 2, after="z_turned0_1")
        fetch_diff(1, 0, "depth0_3")
        subtract(1, 3, "hidden0_3")
        fetch_diff(1, 1, "z0")
        subtract(1, 2, "depth1_3")
        for t in (0, 3, 1, 2):
            shade(1, t)
        quantise_z(1, "bank5")

        late_bank = layer(0, 1, "bank2")
        leave_bank(0, 2, late_bank[:, 0:1, :], "hidden1_2")
        leave_bank(0, 3, late_bank[:, 1:2, :], "z_turned1_1")
        leave_bank(1, 0, layer(1, 0, "bank0")[:])
        leave_bank(1, 2, layer(1, 1, "bank3")[:])
        for t in range(LANES):
            put(0, t)

        out_rows = out_0.rearrange("(p t) u -> p t u", t=LANES)
        pairs = [sbuf([P, 2, PART, 2], BF16, "pairs%d" % q) for q in range(PARTS)]

        def round_rows(copy, t, q):
            copy(pairs[q][:, t // 2, :, t % 2], page[t][:, q * PART : (q + 1) * PART])

        for t in range(LANES):
            put(1, t)
            nc.sync.dma_start(out_rows[:, t, :], page[t][:])
            for q in range(PARTS if t < 2 else SCALAR_PARTS):
                round_rows(nc.scalar.copy, t, q)

        out_bytes = sbuf([P, U], U8, "out_bytes")
        woven = {}

        def weave(copy, q):
            woven[q] = sbuf([P, PART * LANES], BF16, "woven%d" % q)
            copy(
                woven[q][:].bitcast(F32).rearrange("p (s u) -> p s u", u=2),
                pairs[q][:].rearrange("p u s e -> p u (s e)").bitcast(F32).rearrange("p u s -> p s u"),
            )

        def hand_on(q):
            out_words = sbuf([P, PART], U32, "out_words%d" % q)
            nc.vector.quantize_mx(out_words[:].bitcast(FP8X4), out_bytes[:, q * PART : (q + 1) * PART], woven[q][:])
            nc.sync.dma_start(word_rows(out_1)[:, q * PART : (q + 1) * PART], out_words[:].bitcast(I32))

        scalar_parts = list(range(SCALAR_PARTS))
        vector_parts = list(range(SCALAR_PARTS, PARTS))
        for q in scalar_parts:
            weave(nc.scalar.copy, q)
        for t in range(2, LANES):
            for q in vector_parts:
                round_rows(nc.vector.tensor_copy, t, q)
        for q in vector_parts:
            weave(nc.vector.tensor_copy, q)
        for q in vector_parts + scalar_parts:
            hand_on(q)
        for q in range(QUADRANTS):
            queue = nc.sync if q % 2 == 0 else nc.scalar
            queue.dma_start(out_2[0, 4 * q : 4 * q + 4, :].bitcast(I32), out_bytes[32 * q : 32 * q + 4, :].bitcast(I32))
